import numpy as np
import ml_dtypes


def mxq(x, axis, fmt="e4m3"):
    dtype, down = {"e4m3": (ml_dtypes.float8_e4m3fn, 7), "e5m2": (ml_dtypes.float8_e5m2, 14)}[fmt]
    v = np.moveaxis(np.asarray(x, np.float32).astype(ml_dtypes.bfloat16).astype(np.float64), axis, -1)
    blocks = v.reshape(v.shape[:-1] + (-1, 32))
    amax = np.abs(blocks).max(-1, keepdims=True)
    byte = np.maximum(np.where(amax > 0, np.frexp(amax)[1] - 1 + 127, 0) - down, 1)
    scale = np.exp2(byte - 127.0)
    codes = (blocks / scale).astype(np.float32).astype(dtype).astype(np.float64)
    return np.moveaxis((codes * scale).reshape(v.shape), -1, axis)


WIDE = False


def mx_kscale(k):
    if not WIDE:
        return np.ones(k)
    levels = np.array([10, -10, 5, -5, 0])
    if k % 512:
        return np.exp2(np.random.permutation(np.resize(levels, k // 32))).repeat(32)
    a = np.empty((k // 512, 16))
    for p in range(k // 512):
        a[p, :8] = np.random.permutation(np.resize(levels, 8))
        for g in range(8):
            far = levels[np.abs(levels - a[p, g]) >= 10]
            a[p, g + 8] = far[np.random.randint(len(far))]
    return np.exp2(a.ravel()).repeat(32)


def f64(x):
    return np.asarray(x).astype(np.float64)


def striped(idx):
    return np.tile(np.asarray(idx).reshape(-1, 16).T, (8, 1)).astype(np.uint16)


def unstriped(offs):
    return offs[:16].T.reshape(-1).astype(np.int64)


E2M1 = np.array([0.0, 0.5, 1.0, 1.5, 2.0, 3.0, 4.0, 6.0, -0.0, -0.5, -1.0, -1.5, -2.0, -3.0, -4.0, -6.0])


def pack_weight(w, fmt):
    k, n = w.shape
    w = f64(np.asarray(w, np.float32).astype(ml_dtypes.bfloat16)).reshape(k // 32, 32, n)
    amax = np.abs(w).max(1)
    if fmt == "e4m3":
        byte = np.frexp(amax)[1] - 1 + 127 - 7
    else:
        mant, ex = np.frexp(amax / 6.0)
        byte = np.where(mant > 0.5, ex, ex - 1) + 127
    byte = np.clip(np.where(amax > 0, byte, 1), 1, 254)
    scaled = (w * np.exp2(127.0 - byte)[:, None, :]).reshape(k, n).astype(np.float32)
    by_word = np.ascontiguousarray(scaled.reshape(k // 512, 128, 4, n).transpose(0, 1, 3, 2))
    if fmt == "e4m3":
        words = by_word.astype(ml_dtypes.float8_e4m3fn).view(np.uint8)
    else:
        c = by_word.astype(ml_dtypes.float4_e2m1fn).view(np.uint8) & 0xF
        words = (c[..., 0::2] | (c[..., 1::2] << 4)).reshape(k // 512, 128, 2 * n)
    return np.ascontiguousarray(words), np.ascontiguousarray(byte.astype(np.uint8).reshape(k // 512, 16, n))


def unpack_weight(words, scales, fmt):
    g, _, n = scales.shape
    words = np.ascontiguousarray(words).reshape(g, 128, n, -1)
    if fmt == "e4m3":
        vals = words.view(ml_dtypes.float8_e4m3fn).astype(np.float64)
    else:
        nib = np.empty((g, 128, n, 4), np.uint8)
        nib[..., 0::2] = words & 0xF
        nib[..., 1::2] = words >> 4
        vals = E2M1[nib]
    vals = vals * np.repeat(np.exp2(scales.astype(np.float64) - 127.0), 8, axis=1)[..., None]
    return vals.transpose(0, 1, 3, 2).reshape(g * 512, n)


B, N, T, D, NQ = 2, 512, 2048, 1024, 128


def setup_inputs():
    n = np.random.standard_normal
    seg = T // B
    idx = np.concatenate([b * seg + np.random.permutation(seg)[:N] for b in range(B)])
    s = mx_kscale(D)[:, None]
    kp = pack_weight(n((D, T)) / s, "e2m1")
    return {
        "qT": (n((B, D, NQ)) * s * (1.00 / np.sqrt(D))).astype(np.float32),
        "k_words": np.ascontiguousarray(kp[0].reshape(1, 2, 128, T, 2).transpose(0, 2, 3, 1, 4)).reshape(1, 128, T, 4),
        "k_scales": kp[1],
        "kb": np.tile(n(2048), (128, 1)).astype(np.float32),
        "offs": striped(idx),
    }


def reference(qT, k_words, k_scales, kb, offs):
    idx = unstriped(offs)
    pick = lambda x, which: x[:, which].reshape(x.shape[0], B, -1).transpose(1, 0, 2)
    k = unpack_weight(k_words.reshape(1, 128, T, 2, 2).transpose(0, 3, 1, 2, 4).reshape(2, 128, 2 * T), k_scales, "e2m1")
    kg = pick(k, idx)
    qq = mxq(f64(qT), 1, "e4m3")
    a = qq.transpose(0, 2, 1) @ kg
    p = np.square(np.maximum(a + pick(f64(kb), idx)[:, :1, :], 0.0))
    y = p / (np.sum(p, axis=-1, keepdims=True) + 1.0)
    return y

@@ -1,0 +1,185 @@
+from contextlib import ExitStack
+
+import concourse.mybir as mybir
+from concourse.masks import make_identity
+
+B, N, T, D, NQ = 2, 512, 2048, 1024, 128
+FLOPS = 2 * B * N * D * NQ
+
+F32 = mybir.dt.float32
+BF16 = mybir.dt.bfloat16
+I32 = mybir.dt.int32
+U32 = mybir.dt.uint32
+U16 = mybir.dt.uint16
+U8 = mybir.dt.uint8
+FP8X4 = mybir.dt.float8_e4m3fn_x4
+FP4X4 = mybir.dt.float4_e2m1fn_x4
+ALU = mybir.AluOpType
+ACT = mybir.ActivationFunctionType
+
+P = 128
+SEG = T // B
+LC = N // 16
+SHIFT_ROWS = 112
+
+
+def tile_attend_relu2_seg_kernel(tc, qT, k_words, k_scales, kb, offs, out):
+    nc = tc.nc
+    with ExitStack() as ctx:
+        sb = ctx.enter_context(tc.tile_pool(name="sb", bufs=1))
+        ps = ctx.enter_context(tc.psum_pool(name="ps", bufs=1))
+
+        offsets = sb.tile([P, B * LC], U16, name="offsets")
+        word_pool = sb.tile([P, T], I32, name="word_pool", align_bytes=64)
+        scale_pool = sb.tile([P, T], U8, name="scale_pool", align_bytes=64)
+        bias_pool = sb.tile([P, T], F32, name="bias_pool", align_bytes=64)
+        identity = sb.tile([P, P], F32, name="identity")
+        logit1 = sb.tile([P, N + 1], F32, name="logit1")
+        k_scale0 = sb.tile([P, B * N], U8, name="k_scale0", align_bytes=64)
+        k_scale1 = sb.tile([P, B * N], U8, name="k_scale1", align_bytes=64)
+        q_raw = [sb.tile([P, 2, 4 * NQ], F32, name="q_raw%d" % b) for b in range(B)]
+
+        words_hbm = k_words[0].rearrange("p t c -> p (t c)").bitcast(I32)
+
+        def load_scales(b):
+            cols = slice(b * SEG, (b + 1) * SEG)
+            nc.vector.memset(scale_pool[:, cols].bitcast(I32), 0)
+            for row in range(4):
+                nc.sync.dma_start(
+                    scale_pool[row:P:16, cols].bitcast(I32),
+                    k_scales[:, row:16:4, cols].rearrange("o f t -> f o t").bitcast(I32),
+                )
+
+        def load_queries(b):
+            nc.sync.dma_start(q_raw[b][:], qT[b].rearrange("(o p j) q -> p o (j q)", o=2, j=4))
+
+        nc.sync.dma_start(offsets[:], offs)
+        load_scales(0)
+        nc.sync.dma_start(word_pool[:, 0:SEG], words_hbm[:, 0:SEG])
+        nc.sync.dma_start(bias_pool[0:32, 0:SEG], kb[0:32, 0:SEG])
+        load_queries(0)
+        load_scales(1)
+        nc.sync.dma_start(word_pool[:, SEG:T], words_hbm[:, SEG:T])
+        load_queries(1)
+        nc.sync.dma_start(bias_pool[:, SEG:T], kb[:, SEG:T])
+
+        nc.vector.memset(k_scale1[96:128, :].bitcast(I32), 0)
+        nc.vector.memset(bias_pool[32:64, 0:SEG], 0.0)
+        nc.vector.memset(bias_pool[64:128, 0:SEG], 0.0)
+        nc.vector.memset(logit1[:, N : N + 1], 1.0)
+        make_identity(nc, identity[:])
+
+        q_bf = []
+        for b in range(B):
+            t = sb.tile([P, 2, NQ, 4], BF16, name="q_bf%d" % b, align_bytes=64)
+            nc.scalar.copy(t[:], q_raw[b][:].rearrange("p o (j q) -> p o q j", j=4))
+            q_bf.append(t)
+
+        def gather_words(b):
+            pairs = sb.tile([P, N], U32, name="pairs%d" % b, align_bytes=64)
+            nc.vector.tensor_copy(
+                pairs[:],
+                word_pool[:, 0 : (b + 1) * SEG].bitcast(U32).indirect(offsets[:, b * LC : (b + 1) * LC]),
+            )
+            return pairs
+
+        def gather_scales(b):
+            cols = slice(b * N, (b + 1) * N)
+            nc.vector.tensor_copy(
+                k_scale0[:, cols], scale_pool[:, 0 : (b + 1) * SEG].indirect(offsets[:, b * LC : (b + 1) * LC])
+            )
+            nc.sync.dma_start(k_scale1[0:SHIFT_ROWS, cols].bitcast(I32), k_scale0[16:P, cols].bitcast(I32))
+
+        def split_words(b, pairs):
+            k_codes = sb.tile([P, 2, 2 * N], U8, name="k_codes%d" % b, align_bytes=64)
+            for o in range(2):
+                nc.vector.tensor_copy(k_codes[:, o, :].bitcast(U16), pairs[:].bitcast(U16)[:, o : 2 * N : 2])
+            return k_codes
+
+        def quantise(b):
+            codes = sb.tile([P, 2 * NQ], U32, name="q_codes%d" % b, align_bytes=64)
+            scales = sb.tile([P, 2 * NQ], U8, name="q_scales%d" % b, align_bytes=64)
+            nc.vector.quantize_mx(
+                out=codes[:].bitcast(FP8X4),
+                scales=scales[:],
+                in_=q_bf[b][:].rearrange("p o q j -> p (o q j)"),
+            )
+            return codes, scales
+
+        k_scale = (k_scale0, k_scale1)
+        bias = [sb.tile([P, N], F32, name="bias%d" % b) for b in range(B)]
+        weight0 = sb.tile([P, N], F32, name="weight0")
+        weight1 = sb.tile([P, N + 1], F32, name="weight1")
+        result = [sb.tile([P, N], F32, name="result%d" % b) for b in range(B)]
+        total0 = sb.tile([P, 1], F32, name="total0")
+        denom = [sb.tile([P, 1], F32, name="denom%d" % b) for b in range(B)]
+        inv = [sb.tile([P, 1], F32, name="inv%d" % b) for b in range(B)]
+
+        gather_scales(0)
+        pairs0 = gather_words(0)
+        nc.vector.tensor_copy(bias[0][:], bias_pool[:, 0:SEG].indirect(offsets[:, 0:LC]))
+        bias_t = ps.tile([P, 4, P], F32, name="bias_t")
+        for g in range(4):
+            nc.tensor.transpose(bias_t[:, g, :], bias[0][:, g * P : (g + 1) * P], identity[:])
+        bias_col = sb.tile([P, 4], F32, name="bias_col")
+        nc.scalar.copy(bias_col[:], bias_t[:, :, 0])
+
+        k_codes0 = split_words(0, pairs0)
+        qc0, qs0 = quantise(0)
+        gather_scales(1)
+
+        relu_t = sb.tile([P, 4, NQ], F32, name="relu_t")
+        relu0 = ps.tile([P, N], F32, name="relu0")
+        for g in range(4):
+            acc_t = ps.tile([P, NQ], F32, name="acc_t%d" % g)
+            for o in range(2):
+                nc.tensor.matmul_mx(
+                    out=acc_t[:],
+                    lhsT=k_codes0[:, o, 2 * g * P : 2 * (g + 1) * P].bitcast(FP4X4),
+                    lhsT_scale=k_scale[o][:, g * P : (g + 1) * P],
+                    rhs=qc0[:, o * NQ : (o + 1) * NQ].bitcast(FP8X4),
+                    rhs_scale=qs0[:, o * NQ : (o + 1) * NQ],
+                    start=(o == 0),
+                    stop=(o == 1),
+                )
+            nc.scalar.activation(relu_t[:, g, :], acc_t[:], ACT.Relu, bias=bias_col[:, g : g + 1])
+        for g in range(4):
+            nc.tensor.transpose(relu0[:, g * P : (g + 1) * P], relu_t[:, g, :], identity[:])
+        nc.scalar.activation(weight0[:], relu0[:], ACT.Square, accum_out=total0[:])
+        nc.scalar.activation(denom[0][:], total0[:], ACT.Identity, bias=1.0)
+
+        pairs1 = gather_words(1)
+        qc1, qs1 = quantise(1)
+        k_codes1 = split_words(1, pairs1)
+        acc1 = ps.tile([P, N], F32, name="acc1")
+        for o in range(2):
+            nc.tensor.matmul_mx(
+                out=acc1[:],
+                lhsT=qc1[:, o * NQ : (o + 1) * NQ].bitcast(FP8X4),
+                lhsT_scale=qs1[:, o * NQ : (o + 1) * NQ],
+                rhs=k_codes1[:, o, :].bitcast(FP4X4),
+                rhs_scale=k_scale[o][:, N : 2 * N],
+                start=(o == 0),
+                stop=(o == 1),
+            )
+
+        half = N // 2
+        for h in range(2):
+            nc.vector.tensor_copy(
+                bias[1][:, h * half : (h + 1) * half],
+                bias_pool[:].indirect(offsets[:, LC + h * LC // 2 : LC + (h + 1) * LC // 2]),
+            )
+        nc.vector.reciprocal(inv[0][:], denom[0][:])
+        nc.scalar.activation(result[0][:], weight0[:], ACT.Copy, scale=inv[0][:])
+        nc.sync.dma_start(out[0], result[0][:])
+        for h in range(2):
+            cols = slice(h * half, (h + 1) * half)
+            nc.vector.tensor_tensor(logit1[:, cols], acc1[:, cols], bias[1][:, cols], ALU.add)
+        nc.vector.scalar_tensor_tensor(
+            weight1[:], logit1[:], 0.0, logit1[:], ALU.max, ALU.mult, accum_out=denom[1][:]
+        )
+        nc.vector.reciprocal(inv[1][:], denom[1][:])
+        for h, queue in enumerate((nc.sync, nc.scalar)):
+            cols = slice(h * half, (h + 1) * half)
+            nc.vector.tensor_scalar(result[1][:, cols], weight1[:, cols], inv[1][:], None, ALU.mult)
+            queue.dma_start(out[1][:, cols], result[1][:, cols])

@@ -54,25 +54,27 @@ def tile_attend_relu2_seg_kernel(tc, qT, k_words, k_scales, kb, offs, out):
             nc.sync.dma_start(q_raw[b][:], qT[b].rearrange("(o p j) q -> p o (j q)", o=2, j=4))
 
         nc.sync.dma_start(offsets[:], offs)
+        for lo, hi in ((0, 512), (512, SEG)):
+            nc.sync.dma_start(bias_pool[0:32, lo:hi], kb[0:32, lo:hi])
         load_scales(0)
         nc.sync.dma_start(word_pool[:, 0:SEG], words_hbm[:, 0:SEG])
-        nc.sync.dma_start(bias_pool[0:32, 0:SEG], kb[0:32, 0:SEG])
         load_queries(0)
         load_scales(1)
-        nc.sync.dma_start(word_pool[:, SEG:T], words_hbm[:, SEG:T])
         load_queries(1)
+        nc.sync.dma_start(word_pool[:, SEG:T], words_hbm[:, SEG:T])
         nc.sync.dma_start(bias_pool[:, SEG:T], kb[:, SEG:T])
 
-        nc.vector.memset(k_scale1[96:128, :].bitcast(I32), 0)
         nc.vector.memset(bias_pool[32:64, 0:SEG], 0.0)
         nc.vector.memset(bias_pool[64:128, 0:SEG], 0.0)
-        nc.vector.memset(logit1[:, N : N + 1], 1.0)
+        nc.vector.memset(k_scale1[96:128, :].bitcast(I32), 0)
         make_identity(nc, identity[:])
+        nc.scalar.activation(logit1[:, N : N + 1], identity[:, 0:1], ACT.Abs_reciprocal_sqrt, bias=1.0, scale=0.0)
 
         q_bf = []
         for b in range(B):
             t = sb.tile([P, 2, NQ, 4], BF16, name="q_bf%d" % b, align_bytes=64)
-            nc.scalar.copy(t[:], q_raw[b][:].rearrange("p o (j q) -> p o q j", j=4))
+            for o in range(2):
+                nc.scalar.copy(t[:, o, :, :], q_raw[b][:, o, :].rearrange("p (j q) -> p q j", j=4))
             q_bf.append(t)
 
         def gather_words(b):
@@ -88,7 +90,8 @@ def tile_attend_relu2_seg_kernel(tc, qT, k_words, k_scales, kb, offs, out):
             nc.vector.tensor_copy(
                 k_scale0[:, cols], scale_pool[:, 0 : (b + 1) * SEG].indirect(offsets[:, b * LC : (b + 1) * LC])
             )
-            nc.sync.dma_start(k_scale1[0:SHIFT_ROWS, cols].bitcast(I32), k_scale0[16:P, cols].bitcast(I32))
+            for lo, hi in ((0, 64), (64, 96), (96, 112)):
+                nc.scalar.dma_start(k_scale1[lo:hi, cols].bitcast(I32), k_scale0[lo + 16 : hi + 16, cols].bitcast(I32))
 
         def split_words(b, pairs):
             k_codes = sb.tile([P, 2, 2 * N], U8, name="k_codes%d" % b, align_bytes=64)
@@ -115,9 +118,9 @@ def tile_attend_relu2_seg_kernel(tc, qT, k_words, k_scales, kb, offs, out):
         denom = [sb.tile([P, 1], F32, name="denom%d" % b) for b in range(B)]
         inv = [sb.tile([P, 1], F32, name="inv%d" % b) for b in range(B)]
 
+        nc.vector.tensor_copy(bias[0][:], bias_pool[:, 0:SEG].indirect(offsets[:, 0:LC]))
         gather_scales(0)
         pairs0 = gather_words(0)
-        nc.vector.tensor_copy(bias[0][:], bias_pool[:, 0:SEG].indirect(offsets[:, 0:LC]))
         bias_t = ps.tile([P, 4, P], F32, name="bias_t")
         for g in range(4):
             nc.tensor.transpose(bias_t[:, g, :], bias[0][:, g * P : (g + 1) * P], identity[:])
@@ -131,7 +134,7 @@ def tile_attend_relu2_seg_kernel(tc, qT, k_words, k_scales, kb, offs, out):
         relu_t = sb.tile([P, 4, NQ], F32, name="relu_t")
         relu0 = ps.tile([P, N], F32, name="relu0")
         for g in range(4):
-            acc_t = ps.tile([P, NQ], F32, name="acc_t%d" % g)
+            acc_t = ps.tile([P, NQ], F32, name="acc_t%d" % g, tag="bank%d" % g)
             for o in range(2):
                 nc.tensor.matmul_mx(
                     out=acc_t[:],
@@ -146,12 +149,14 @@ def tile_attend_relu2_seg_kernel(tc, qT, k_words, k_scales, kb, offs, out):
         for g in range(4):
             nc.tensor.transpose(relu0[:, g * P : (g + 1) * P], relu_t[:, g, :], identity[:])
         nc.scalar.activation(weight0[:], relu0[:], ACT.Square, accum_out=total0[:])
-        nc.scalar.activation(denom[0][:], total0[:], ACT.Identity, bias=1.0)
+        nc.scalar.activation(inv[0][:], total0[:], ACT.Abs_reciprocal_sqrt, bias=1.0)
+        nc.scalar.activation(result[0][:], relu0[:], ACT.Square, scale=inv[0][:])
+        nc.sync.dma_start(out[0], result[0][:])
 
         pairs1 = gather_words(1)
         qc1, qs1 = quantise(1)
         k_codes1 = split_words(1, pairs1)
-        acc1 = ps.tile([P, N], F32, name="acc1")
+        acc1 = ps.tile([P, N], F32, name="acc1", tag="bank0")
         for o in range(2):
             nc.tensor.matmul_mx(
                 out=acc1[:],
@@ -169,9 +174,6 @@ def tile_attend_relu2_seg_kernel(tc, qT, k_words, k_scales, kb, offs, out):
                 bias[1][:, h * half : (h + 1) * half],
                 bias_pool[:].indirect(offsets[:, LC + h * LC // 2 : LC + (h + 1) * LC // 2]),
             )
-        nc.vector.reciprocal(inv[0][:], denom[0][:])
-        nc.scalar.activation(result[0][:], weight0[:], ACT.Copy, scale=inv[0][:])
-        nc.sync.dma_start(out[0], result[0][:])
         for h in range(2):
             cols = slice(h * half, (h + 1) * half)
             nc.vector.tensor_tensor(logit1[:, cols], acc1[:, cols], bias[1][:, cols], ALU.add)

@@ -20,7 +20,7 @@ ACT = mybir.ActivationFunctionType
 P = 128
 SEG = T // B
 LC = N // 16
-SHIFT_ROWS = 112
+SCALAR_COLS = 192
 
 
 def tile_attend_relu2_seg_kernel(tc, qT, k_words, k_scales, kb, offs, out):
@@ -53,6 +53,11 @@ def tile_attend_relu2_seg_kernel(tc, qT, k_words, k_scales, kb, offs, out):
         def load_queries(b):
             nc.sync.dma_start(q_raw[b][:], qT[b].rearrange("(o p j) q -> p o (j q)", o=2, j=4))
 
+        one = sb.tile([P, 1], F32, name="one")
+        nc.gpsimd.memset(one[:], 1.0)
+        nc.scalar.activation(logit1[:, N : N + 1], one[:], ACT.Abs_reciprocal_sqrt)
+        make_identity(nc, identity[:])
+
         nc.sync.dma_start(offsets[:], offs)
         for lo, hi in ((0, 512), (512, SEG)):
             nc.sync.dma_start(bias_pool[0:32, lo:hi], kb[0:32, lo:hi])
@@ -67,14 +72,15 @@ def tile_attend_relu2_seg_kernel(tc, qT, k_words, k_scales, kb, offs, out):
         nc.vector.memset(bias_pool[32:64, 0:SEG], 0.0)
         nc.vector.memset(bias_pool[64:128, 0:SEG], 0.0)
         nc.vector.memset(k_scale1[96:128, :].bitcast(I32), 0)
-        make_identity(nc, identity[:])
-        nc.scalar.activation(logit1[:, N : N + 1], identity[:, 0:1], ACT.Abs_reciprocal_sqrt, bias=1.0, scale=0.0)
 
         q_bf = []
         for b in range(B):
             t = sb.tile([P, 2, NQ, 4], BF16, name="q_bf%d" % b, align_bytes=64)
             for o in range(2):
-                nc.scalar.copy(t[:, o, :, :], q_raw[b][:, o, :].rearrange("p (j q) -> p q j", j=4))
+                nc.scalar.copy(
+                    t[:, o, :, :].rearrange("p (c i) j -> p c j i", i=4),
+                    q_raw[b][:, o, :].rearrange("p (j c i) -> p c j i", j=4, i=4),
+                )
             q_bf.append(t)
 
         def gather_words(b):
@@ -174,14 +180,25 @@ def tile_attend_relu2_seg_kernel(tc, qT, k_words, k_scales, kb, offs, out):
                 bias[1][:, h * half : (h + 1) * half],
                 bias_pool[:].indirect(offsets[:, LC + h * LC // 2 : LC + (h + 1) * LC // 2]),
             )
-        for h in range(2):
-            cols = slice(h * half, (h + 1) * half)
+        head, rest = slice(0, SCALAR_COLS), slice(SCALAR_COLS, N)
+        rest_and_one = slice(SCALAR_COLS, N + 1)
+        for cols in (head, rest):
             nc.vector.tensor_tensor(logit1[:, cols], acc1[:, cols], bias[1][:, cols], ALU.add)
+        relu1 = sb.tile([P, SCALAR_COLS], F32, name="relu1")
+        total_head = sb.tile([P, 1], F32, name="total_head")
+        nc.scalar.activation(relu1[:], logit1[:, head], ACT.Relu)
+        nc.scalar.activation(weight1[:, head], relu1[:], ACT.Square, accum_out=total_head[:])
         nc.vector.scalar_tensor_tensor(
-            weight1[:], logit1[:], 0.0, logit1[:], ALU.max, ALU.mult, accum_out=denom[1][:]
+            weight1[:, rest_and_one],
+            logit1[:, rest_and_one],
+            0.0,
+            logit1[:, rest_and_one],
+            ALU.max,
+            ALU.mult,
+            accum_out=denom[1][:],
         )
-        nc.vector.reciprocal(inv[1][:], denom[1][:])
-        for h, queue in enumerate((nc.sync, nc.scalar)):
-            cols = slice(h * half, (h + 1) * half)
-            nc.vector.tensor_scalar(result[1][:, cols], weight1[:, cols], inv[1][:], None, ALU.mult)
-            queue.dma_start(out[1][:, cols], result[1][:, cols])
+        nc.scalar.activation(inv[1][:], denom[1][:], ACT.Abs_reciprocal_sqrt, bias=total_head[:])
+        nc.vector.tensor_scalar(result[1][:, rest], weight1[:, rest], inv[1][:], inv[1][:], ALU.mult, ALU.mult)
+        nc.sync.dma_start(out[1][:, rest], result[1][:, rest])
+        nc.scalar.activation(result[1][:, head], relu1[:], ACT.Square, scale=inv[1][:])
+        nc.scalar.dma_start(out[1][:, head], result[1][:, head])

@@ -28,10 +28,14 @@ def tile_attend_relu2_seg_kernel(tc, qT, k_words, k_scales, kb, offs, out):
     with ExitStack() as ctx:
         sb = ctx.enter_context(tc.tile_pool(name="sb", bufs=1))
         ps = ctx.enter_context(tc.psum_pool(name="ps", bufs=1))
+        reused = ctx.enter_context(tc.tile_pool(name="reused", bufs=1))
 
         offsets = sb.tile([P, B * LC], U16, name="offsets")
         word_pool = sb.tile([P, T], I32, name="word_pool", align_bytes=64)
-        scale_pool = sb.tile([P, T], U8, name="scale_pool", align_bytes=64)
+        scale_pool = [
+            reused.tile([P, SEG], U8, name="scale_pool0", align_bytes=64, offset=1024),
+            reused.tile([P, T], U8, name="scale_pool1", align_bytes=64, offset=8192),
+        ]
         bias_pool = sb.tile([P, T], F32, name="bias_pool", align_bytes=64)
         identity = sb.tile([P, P], F32, name="identity")
         logit1 = sb.tile([P, N + 1], F32, name="logit1")
@@ -43,10 +47,10 @@ def tile_attend_relu2_seg_kernel(tc, qT, k_words, k_scales, kb, offs, out):
 
         def load_scales(b):
             cols = slice(b * SEG, (b + 1) * SEG)
-            nc.vector.memset(scale_pool[:, cols].bitcast(I32), 0)
+            nc.vector.memset(scale_pool[b][:, cols].bitcast(I32), 0)
             for row in range(4):
                 nc.sync.dma_start(
-                    scale_pool[row:P:16, cols].bitcast(I32),
+                    scale_pool[b][row:P:16, cols].bitcast(I32),
                     k_scales[:, row:16:4, cols].rearrange("o f t -> f o t").bitcast(I32),
                 )
 
@@ -84,7 +88,7 @@ def tile_attend_relu2_seg_kernel(tc, qT, k_words, k_scales, kb, offs, out):
             q_bf.append(t)
 
         def gather_words(b):
-            pairs = sb.tile([P, N], U32, name="pairs%d" % b, align_bytes=64)
+            pairs = reused.tile([P, N], U32, name="pairs%d" % b, align_bytes=64, offset=10752 - 2048 * b)
             nc.vector.tensor_copy(
                 pairs[:],
                 word_pool[:, 0 : (b + 1) * SEG].bitcast(U32).indirect(offsets[:, b * LC : (b + 1) * LC]),
@@ -94,19 +98,19 @@ def tile_attend_relu2_seg_kernel(tc, qT, k_words, k_scales, kb, offs, out):
         def gather_scales(b):
             cols = slice(b * N, (b + 1) * N)
             nc.vector.tensor_copy(
-                k_scale0[:, cols], scale_pool[:, 0 : (b + 1) * SEG].indirect(offsets[:, b * LC : (b + 1) * LC])
+                k_scale0[:, cols], scale_pool[b][:].indirect(offsets[:, b * LC : (b + 1) * LC])
             )
             for lo, hi in ((0, 64), (64, 96), (96, 112)):
                 nc.scalar.dma_start(k_scale1[lo:hi, cols].bitcast(I32), k_scale0[lo + 16 : hi + 16, cols].bitcast(I32))
 
         def split_words(b, pairs):
-            k_codes = sb.tile([P, 2, 2 * N], U8, name="k_codes%d" % b, align_bytes=64)
+            k_codes = reused.tile([P, 2, 2 * N], U8, name="k_codes%d" % b, align_bytes=64, offset=1536 + 2048 * b)
             for o in range(2):
                 nc.vector.tensor_copy(k_codes[:, o, :].bitcast(U16), pairs[:].bitcast(U16)[:, o : 2 * N : 2])
             return k_codes
 
         def quantise(b):
-            codes = sb.tile([P, 2 * NQ], U32, name="q_codes%d" % b, align_bytes=64)
+            codes = reused.tile([P, 2 * NQ], U32, name="q_codes%d" % b, align_bytes=64, offset=7680 - 2048 * b)
             scales = sb.tile([P, 2 * NQ], U8, name="q_scales%d" % b, align_bytes=64)
             nc.vector.quantize_mx(
                 out=codes[:].bitcast(FP8X4),

@@ -31,86 +31,77 @@ def tile_attend_relu2_seg_kernel(tc, qT, k_words, k_scales, kb, offs, out):
         reused = ctx.enter_context(tc.tile_pool(name="reused", bufs=1))
 
         offsets = sb.tile([P, B * LC], U16, name="offsets")
-        word_pool = sb.tile([P, T], I32, name="word_pool", align_bytes=64)
-        scale_pool = [
-            reused.tile([P, SEG], U8, name="scale_pool0", align_bytes=64, offset=1024),
-            reused.tile([P, T], U8, name="scale_pool1", align_bytes=64, offset=8192),
+        word_pool = [
+            reused.tile([P, (b + 1) * SEG], I32, name="word_pool%d" % b, align_bytes=64, offset=(4096, 10240)[b])
+            for b in range(B)
         ]
-        bias_pool = sb.tile([P, T], F32, name="bias_pool", align_bytes=64)
+        bias_pool = [
+            reused.tile([P, SEG], F32, name="bias_pool0", align_bytes=64, offset=20480),
+            sb.tile([P, T], F32, name="bias_pool1", align_bytes=64),
+        ]
+        scale_pool = sb.tile([P, T], U8, name="scale_pool", align_bytes=64)
+        scale_listed = sb.tile([P, B * N], U8, name="scale_listed", align_bytes=64)
+        k_scale = [sb.tile([P, B * N], U8, name="k_scale%d" % o, align_bytes=64) for o in range(2)]
         identity = sb.tile([P, P], F32, name="identity")
         logit1 = sb.tile([P, N + 1], F32, name="logit1")
-        k_scale0 = sb.tile([P, B * N], U8, name="k_scale0", align_bytes=64)
-        k_scale1 = sb.tile([P, B * N], U8, name="k_scale1", align_bytes=64)
-        q_raw = [sb.tile([P, 2, 4 * NQ], F32, name="q_raw%d" % b) for b in range(B)]
+        q_raw = [
+            sb.tile([P, 2, 4 * NQ], F32, name="q_raw0"),
+            reused.tile([P, 2, 4 * NQ], F32, name="q_raw1", align_bytes=64, offset=0),
+        ]
 
         words_hbm = k_words[0].rearrange("p t c -> p (t c)").bitcast(I32)
+        scale_rows = k_scales.rearrange("o (h e j) t -> e (o h) j t", h=2, e=2, j=4)
 
-        def load_scales(b):
+        nc.sync.dma_start(offsets[:], offs)
+        for e in range(2):
+            nc.sync.dma_start(scale_pool[16 + 32 * e : 32 + 32 * e, :].bitcast(I32), scale_rows[e].bitcast(I32))
+        nc.sync.dma_start(bias_pool[0][P - 1 : P, :], kb[0:1, 0:SEG])
+        for b in range(B):
             cols = slice(b * SEG, (b + 1) * SEG)
-            nc.vector.memset(scale_pool[b][:, cols].bitcast(I32), 0)
-            for row in range(4):
-                nc.sync.dma_start(
-                    scale_pool[b][row:P:16, cols].bitcast(I32),
-                    k_scales[:, row:16:4, cols].rearrange("o f t -> f o t").bitcast(I32),
-                )
-
-        def load_queries(b):
             nc.sync.dma_start(q_raw[b][:], qT[b].rearrange("(o p j) q -> p o (j q)", o=2, j=4))
+            nc.sync.dma_start(word_pool[b][:, cols], words_hbm[:, cols])
+        nc.sync.dma_start(bias_pool[1][:, SEG:T], kb[:, SEG:T])
+
+        for lo, hi in ((0, 16), (32, 48), (64, P)):
+            nc.vector.memset(scale_pool[lo:hi, :].bitcast(I32), 0)
+        nc.vector.memset(bias_pool[0][0 : P - 1, :], 0.0)
 
         one = sb.tile([P, 1], F32, name="one")
         nc.gpsimd.memset(one[:], 1.0)
         nc.scalar.activation(logit1[:, N : N + 1], one[:], ACT.Abs_reciprocal_sqrt)
         make_identity(nc, identity[:])
 
-        nc.sync.dma_start(offsets[:], offs)
-        for lo, hi in ((0, 512), (512, SEG)):
-            nc.sync.dma_start(bias_pool[0:32, lo:hi], kb[0:32, lo:hi])
-        load_scales(0)
-        nc.sync.dma_start(word_pool[:, 0:SEG], words_hbm[:, 0:SEG])
-        load_queries(0)
-        load_scales(1)
-        load_queries(1)
-        nc.sync.dma_start(word_pool[:, SEG:T], words_hbm[:, SEG:T])
-        nc.sync.dma_start(bias_pool[:, SEG:T], kb[:, SEG:T])
-
-        nc.vector.memset(bias_pool[32:64, 0:SEG], 0.0)
-        nc.vector.memset(bias_pool[64:128, 0:SEG], 0.0)
-        nc.vector.memset(k_scale1[96:128, :].bitcast(I32), 0)
+        nc.vector.tensor_copy(scale_listed[:], scale_pool[:].indirect(offsets[:]))
+        for o in range(2):
+            for h in range(2):
+                first = 16 + 4 * (2 * o + h)
+                nc.scalar.dma_start(
+                    k_scale[o][64 * h : 64 * h + 64, :].bitcast(I32),
+                    scale_listed[first : first + 64, :].bitcast(I32),
+                )
 
         q_bf = []
         for b in range(B):
-            t = sb.tile([P, 2, NQ, 4], BF16, name="q_bf%d" % b, align_bytes=64)
-            for o in range(2):
-                nc.scalar.copy(
-                    t[:, o, :, :].rearrange("p (c i) j -> p c j i", i=4),
-                    q_raw[b][:, o, :].rearrange("p (j c i) -> p c j i", j=4, i=4),
-                )
+            t = reused.tile([P, 2, NQ, 4], BF16, name="q_bf%d" % b, align_bytes=64, offset=(8192, 18432)[b])
+            nc.scalar.copy(
+                t[:].rearrange("p o (c i) j -> p o c j i", i=4),
+                q_raw[b][:].rearrange("p o (j c i) -> p o c j i", j=4, i=4),
+            )
             q_bf.append(t)
 
         def gather_words(b):
-            pairs = reused.tile([P, N], U32, name="pairs%d" % b, align_bytes=64, offset=10752 - 2048 * b)
-            nc.vector.tensor_copy(
-                pairs[:],
-                word_pool[:, 0 : (b + 1) * SEG].bitcast(U32).indirect(offsets[:, b * LC : (b + 1) * LC]),
-            )
+            pairs = reused.tile([P, N], U32, name="pairs%d" % b, align_bytes=64, offset=(24576, 7168)[b])
+            nc.vector.tensor_copy(pairs[:], word_pool[b][:].bitcast(U32).indirect(offsets[:, b * LC : (b + 1) * LC]))
             return pairs
 
-        def gather_scales(b):
-            cols = slice(b * N, (b + 1) * N)
-            nc.vector.tensor_copy(
-                k_scale0[:, cols], scale_pool[b][:].indirect(offsets[:, b * LC : (b + 1) * LC])
-            )
-            for lo, hi in ((0, 64), (64, 96), (96, 112)):
-                nc.scalar.dma_start(k_scale1[lo:hi, cols].bitcast(I32), k_scale0[lo + 16 : hi + 16, cols].bitcast(I32))
-
         def split_words(b, pairs):
-            k_codes = reused.tile([P, 2, 2 * N], U8, name="k_codes%d" % b, align_bytes=64, offset=1536 + 2048 * b)
+            k_codes = reused.tile([P, 2, 2 * N], U8, name="k_codes%d" % b, align_bytes=64, offset=(29696, 26624)[b])
             for o in range(2):
                 nc.vector.tensor_copy(k_codes[:, o, :].bitcast(U16), pairs[:].bitcast(U16)[:, o : 2 * N : 2])
             return k_codes
 
         def quantise(b):
-            codes = reused.tile([P, 2 * NQ], U32, name="q_codes%d" % b, align_bytes=64, offset=7680 - 2048 * b)
+            codes = reused.tile([P, 2 * NQ], U32, name="q_codes%d" % b, align_bytes=64, offset=(22528, 28672)[b])
             scales = sb.tile([P, 2 * NQ], U8, name="q_scales%d" % b, align_bytes=64)
             nc.vector.quantize_mx(
                 out=codes[:].bitcast(FP8X4),
@@ -119,27 +110,27 @@ def tile_attend_relu2_seg_kernel(tc, qT, k_words, k_scales, kb, offs, out):
             )
             return codes, scales
 
-        k_scale = (k_scale0, k_scale1)
-        bias = [sb.tile([P, N], F32, name="bias%d" % b) for b in range(B)]
+        bias = [
+            reused.tile([P, N], F32, name="bias0", align_bytes=64, offset=29696),
+            reused.tile([P, N], F32, name="bias1", align_bytes=64, offset=17408),
+        ]
         weight0 = sb.tile([P, N], F32, name="weight0")
         weight1 = sb.tile([P, N + 1], F32, name="weight1")
         result = [sb.tile([P, N], F32, name="result%d" % b) for b in range(B)]
         total0 = sb.tile([P, 1], F32, name="total0")
-        denom = [sb.tile([P, 1], F32, name="denom%d" % b) for b in range(B)]
+        denom1 = sb.tile([P, 1], F32, name="denom1")
         inv = [sb.tile([P, 1], F32, name="inv%d" % b) for b in range(B)]
 
-        nc.vector.tensor_copy(bias[0][:], bias_pool[:, 0:SEG].indirect(offsets[:, 0:LC]))
-        gather_scales(0)
+        nc.vector.tensor_copy(bias[0][:], bias_pool[0][:].indirect(offsets[:, 0:LC]))
         pairs0 = gather_words(0)
         bias_t = ps.tile([P, 4, P], F32, name="bias_t")
         for g in range(4):
             nc.tensor.transpose(bias_t[:, g, :], bias[0][:, g * P : (g + 1) * P], identity[:])
-        bias_col = sb.tile([P, 4], F32, name="bias_col")
-        nc.scalar.copy(bias_col[:], bias_t[:, :, 0])
+        bias_col = reused.tile([P, 4], F32, name="bias_col", align_bytes=64, offset=0)
+        nc.scalar.copy(bias_col[:], bias_t[:, :, P - 1])
 
-        k_codes0 = split_words(0, pairs0)
         qc0, qs0 = quantise(0)
-        gather_scales(1)
+        k_codes0 = split_words(0, pairs0)
 
         relu_t = sb.tile([P, 4, NQ], F32, name="relu_t")
         relu0 = ps.tile([P, N], F32, name="relu0")
@@ -166,7 +157,7 @@ def tile_attend_relu2_seg_kernel(tc, qT, k_words, k_scales, kb, offs, out):
         pairs1 = gather_words(1)
         qc1, qs1 = quantise(1)
         k_codes1 = split_words(1, pairs1)
-        acc1 = ps.tile([P, N], F32, name="acc1", tag="bank0")
+        acc1 = ps.tile([P, N], F32, name="acc1", tag="bank3")
         for o in range(2):
             nc.tensor.matmul_mx(
                 out=acc1[:],
@@ -182,7 +173,7 @@ def tile_attend_relu2_seg_kernel(tc, qT, k_words, k_scales, kb, offs, out):
         for h in range(2):
             nc.vector.tensor_copy(
                 bias[1][:, h * half : (h + 1) * half],
-                bias_pool[:].indirect(offsets[:, LC + h * LC // 2 : LC + (h + 1) * LC // 2]),
+                bias_pool[1][:].indirect(offsets[:, LC + h * LC // 2 : LC + (h + 1) * LC // 2]),
             )
         head, rest = slice(0, SCALAR_COLS), slice(SCALAR_COLS, N)
         rest_and_one = slice(SCALAR_COLS, N + 1)
@@ -199,9 +190,9 @@ def tile_attend_relu2_seg_kernel(tc, qT, k_words, k_scales, kb, offs, out):
             logit1[:, rest_and_one],
             ALU.max,
             ALU.mult,
-            accum_out=denom[1][:],
+            accum_out=denom1[:],
         )
-        nc.scalar.activation(inv[1][:], denom[1][:], ACT.Abs_reciprocal_sqrt, bias=total_head[:])
+        nc.scalar.activation(inv[1][:], denom1[:], ACT.Abs_reciprocal_sqrt, bias=total_head[:])
         nc.vector.tensor_scalar(result[1][:, rest], weight1[:, rest], inv[1][:], inv[1][:], ALU.mult, ALU.mult)
         nc.sync.dma_start(out[1][:, rest], result[1][:, rest])
         nc.scalar.activation(result[1][:, head], relu1[:], ACT.Square, scale=inv[1][:])

@@ -20,7 +20,6 @@ ACT = mybir.ActivationFunctionType
 P = 128
 SEG = T // B
 LC = N // 16
-SCALAR_COLS = 192
 
 
 def tile_attend_relu2_seg_kernel(tc, qT, k_words, k_scales, kb, offs, out):
@@ -118,7 +117,6 @@ def tile_attend_relu2_seg_kernel(tc, qT, k_words, k_scales, kb, offs, out):
         weight1 = sb.tile([P, N + 1], F32, name="weight1")
         result = [sb.tile([P, N], F32, name="result%d" % b) for b in range(B)]
         total0 = sb.tile([P, 1], F32, name="total0")
-        denom1 = sb.tile([P, 1], F32, name="denom1")
         inv = [sb.tile([P, 1], F32, name="inv%d" % b) for b in range(B)]
 
         nc.vector.tensor_copy(bias[0][:], bias_pool[0][:].indirect(offsets[:, 0:LC]))
@@ -157,43 +155,38 @@ def tile_attend_relu2_seg_kernel(tc, qT, k_words, k_scales, kb, offs, out):
         pairs1 = gather_words(1)
         qc1, qs1 = quantise(1)
         k_codes1 = split_words(1, pairs1)
-        acc1 = ps.tile([P, N], F32, name="acc1", tag="bank3")
-        for o in range(2):
-            nc.tensor.matmul_mx(
-                out=acc1[:],
-                lhsT=qc1[:, o * NQ : (o + 1) * NQ].bitcast(FP8X4),
-                lhsT_scale=qs1[:, o * NQ : (o + 1) * NQ],
-                rhs=k_codes1[:, o, :].bitcast(FP4X4),
-                rhs_scale=k_scale[o][:, N : 2 * N],
-                start=(o == 0),
-                stop=(o == 1),
-            )
-
         half = N // 2
+        acc1 = [ps.tile([P, half], F32, name="acc1%d" % h, tag="bank%d" % (3 - h)) for h in range(2)]
+        for g in range(4):
+            keys = slice(g * P, (g + 1) * P)
+            for o in range(2):
+                nc.tensor.matmul_mx(
+                    out=acc1[g // 2][:, (g % 2) * P : (g % 2 + 1) * P],
+                    lhsT=qc1[:, o * NQ : (o + 1) * NQ].bitcast(FP8X4),
+                    lhsT_scale=qs1[:, o * NQ : (o + 1) * NQ],
+                    rhs=k_codes1[:, o, 2 * g * P : 2 * (g + 1) * P].bitcast(FP4X4),
+                    rhs_scale=k_scale[o][:, N + g * P : N + (g + 1) * P],
+                    start=(o == 0),
+                    stop=(o == 1),
+                )
+
         for h in range(2):
             nc.vector.tensor_copy(
                 bias[1][:, h * half : (h + 1) * half],
                 bias_pool[1][:].indirect(offsets[:, LC + h * LC // 2 : LC + (h + 1) * LC // 2]),
             )
-        head, rest = slice(0, SCALAR_COLS), slice(SCALAR_COLS, N)
-        rest_and_one = slice(SCALAR_COLS, N + 1)
-        for cols in (head, rest):
-            nc.vector.tensor_tensor(logit1[:, cols], acc1[:, cols], bias[1][:, cols], ALU.add)
-        relu1 = sb.tile([P, SCALAR_COLS], F32, name="relu1")
-        total_head = sb.tile([P, 1], F32, name="total_head")
-        nc.scalar.activation(relu1[:], logit1[:, head], ACT.Relu)
-        nc.scalar.activation(weight1[:, head], relu1[:], ACT.Square, accum_out=total_head[:])
-        nc.vector.scalar_tensor_tensor(
-            weight1[:, rest_and_one],
-            logit1[:, rest_and_one],
-            0.0,
-            logit1[:, rest_and_one],
-            ALU.max,
-            ALU.mult,
-            accum_out=denom1[:],
-        )
-        nc.scalar.activation(inv[1][:], denom1[:], ACT.Abs_reciprocal_sqrt, bias=total_head[:])
-        nc.vector.tensor_scalar(result[1][:, rest], weight1[:, rest], inv[1][:], inv[1][:], ALU.mult, ALU.mult)
-        nc.sync.dma_start(out[1][:, rest], result[1][:, rest])
-        nc.scalar.activation(result[1][:, head], relu1[:], ACT.Square, scale=inv[1][:])
-        nc.scalar.dma_start(out[1][:, head], result[1][:, head])
+        halves = (slice(0, half), slice(half, N))
+        summed = (slice(0, half), slice(half, N + 1))
+        part = [sb.tile([P, 1], F32, name="part%d" % h) for h in range(2)]
+        for h in range(2):
+            nc.vector.tensor_tensor(logit1[:, halves[h]], acc1[h][:], bias[1][:, halves[h]], ALU.add)
+        for h in range(2):
+            cols = summed[h]
+            nc.vector.scalar_tensor_tensor(
+                weight1[:, cols], logit1[:, cols], 0.0, logit1[:, cols], ALU.max, ALU.mult, accum_out=part[h][:]
+            )
+        nc.scalar.activation(inv[1][:], part[1][:], ACT.Abs_reciprocal_sqrt, bias=part[0][:])
+        for h, queue in enumerate((nc.sync, nc.scalar)):
+            cols = halves[h]
+            nc.vector.tensor_scalar(result[1][:, cols], weight1[:, cols], inv[1][:], inv[1][:], ALU.mult, ALU.mult)
+            queue.dma_start(out[1][:, cols], result[1][:, cols])

@@ -39,12 +39,14 @@ def tile_attend_relu2_seg_kernel(tc, qT, k_words, k_scales, kb, offs, out):
             sb.tile([P, T], F32, name="bias_pool1", align_bytes=64),
         ]
         scale_pool = sb.tile([P, T], U8, name="scale_pool", align_bytes=64)
-        scale_listed = sb.tile([P, B * N], U8, name="scale_listed", align_bytes=64)
-        k_scale = [sb.tile([P, B * N], U8, name="k_scale%d" % o, align_bytes=64) for o in range(2)]
+        scale_listed = [sb.tile([P, N], U8, name="scale_listed%d" % b, align_bytes=64) for b in range(B)]
+        k_scale = [
+            [sb.tile([P, N], U8, name="k_scale%d%d" % (b, o), align_bytes=64) for o in range(2)] for b in range(B)
+        ]
         identity = sb.tile([P, P], F32, name="identity")
         logit1 = sb.tile([P, N + 1], F32, name="logit1")
         q_raw = [
-            sb.tile([P, 2, 4 * NQ], F32, name="q_raw0"),
+            reused.tile([P, 2, 4 * NQ], F32, name="q_raw0", align_bytes=64, offset=36864),
             reused.tile([P, 2, 4 * NQ], F32, name="q_raw1", align_bytes=64, offset=0),
         ]
 
@@ -52,32 +54,40 @@ def tile_attend_relu2_seg_kernel(tc, qT, k_words, k_scales, kb, offs, out):
         scale_rows = k_scales.rearrange("o (h e j) t -> e (o h) j t", h=2, e=2, j=4)
 
         nc.sync.dma_start(offsets[:], offs)
+        nc.sync.dma_start(bias_pool[0][P - 1 : P, :], kb[0:1, 0:SEG])
         for e in range(2):
             nc.sync.dma_start(scale_pool[16 + 32 * e : 32 + 32 * e, :].bitcast(I32), scale_rows[e].bitcast(I32))
-        nc.sync.dma_start(bias_pool[0][P - 1 : P, :], kb[0:1, 0:SEG])
         for b in range(B):
             cols = slice(b * SEG, (b + 1) * SEG)
             nc.sync.dma_start(q_raw[b][:], qT[b].rearrange("(o p j) q -> p o (j q)", o=2, j=4))
             nc.sync.dma_start(word_pool[b][:, cols], words_hbm[:, cols])
-        nc.sync.dma_start(bias_pool[1][:, SEG:T], kb[:, SEG:T])
 
+        nc.vector.memset(bias_pool[0][0 : P - 1, :], 0.0)
         for lo, hi in ((0, 16), (32, 48), (64, P)):
             nc.vector.memset(scale_pool[lo:hi, :].bitcast(I32), 0)
-        nc.vector.memset(bias_pool[0][0 : P - 1, :], 0.0)
 
         one = sb.tile([P, 1], F32, name="one")
         nc.gpsimd.memset(one[:], 1.0)
         nc.scalar.activation(logit1[:, N : N + 1], one[:], ACT.Abs_reciprocal_sqrt)
         make_identity(nc, identity[:])
 
-        nc.vector.tensor_copy(scale_listed[:], scale_pool[:].indirect(offsets[:]))
-        for o in range(2):
-            for h in range(2):
-                first = 16 + 4 * (2 * o + h)
-                nc.scalar.dma_start(
-                    k_scale[o][64 * h : 64 * h + 64, :].bitcast(I32),
-                    scale_listed[first : first + 64, :].bitcast(I32),
-                )
+        half = N // 2
+        bias0 = [
+            reused.tile([P, half], F32, name="bias0%d" % h, align_bytes=64, offset=(29696, 36864)[h]) for h in range(2)
+        ]
+        nc.vector.tensor_copy(bias0[0][:], bias_pool[0][:].indirect(offsets[:, 0 : LC // 2]))
+        for b in range(B):
+            nc.vector.tensor_copy(scale_listed[b][:], scale_pool[:].indirect(offsets[:, b * LC : (b + 1) * LC]))
+
+        for b, queue in enumerate((nc.scalar, nc.sync)):
+            for o in range(2):
+                for h in range(2):
+                    first = 16 + 4 * (2 * o + h)
+                    queue.dma_start(
+                        k_scale[b][o][64 * h : 64 * h + 64, :].bitcast(I32),
+                        scale_listed[b][first : first + 64, :].bitcast(I32),
+                    )
+        nc.sync.dma_start(bias_pool[1][:, SEG:T], kb[:, SEG:T])
 
         q_bf = []
         for b in range(B):
@@ -94,13 +104,20 @@ def tile_attend_relu2_seg_kernel(tc, qT, k_words, k_scales, kb, offs, out):
             return pairs
 
         def split_words(b, pairs):
-            k_codes = reused.tile([P, 2, 2 * N], U8, name="k_codes%d" % b, align_bytes=64, offset=(29696, 26624)[b])
-            for o in range(2):
-                nc.vector.tensor_copy(k_codes[:, o, :].bitcast(U16), pairs[:].bitcast(U16)[:, o : 2 * N : 2])
+            k_codes = []
+            for h in range(2):
+                t = reused.tile(
+                    [P, 2, N], U8, name="k_codes%d%d" % (b, h), align_bytes=64, offset=(20480, 26624)[b] + 1024 * h
+                )
+                nc.vector.tensor_copy(
+                    t[:].rearrange("p o c -> p (o c)").bitcast(U16).rearrange("p (o n) -> p o n", o=2),
+                    pairs[:, h * N // 2 : (h + 1) * N // 2].bitcast(U16).rearrange("p (n o) -> p o n", o=2),
+                )
+                k_codes.append(t)
             return k_codes
 
         def quantise(b):
-            codes = reused.tile([P, 2 * NQ], U32, name="q_codes%d" % b, align_bytes=64, offset=(22528, 28672)[b])
+            codes = reused.tile([P, 2 * NQ], U32, name="q_codes%d" % b, align_bytes=64, offset=(40960, 28672)[b])
             scales = sb.tile([P, 2 * NQ], U8, name="q_scales%d" % b, align_bytes=64)
             nc.vector.quantize_mx(
                 out=codes[:].bitcast(FP8X4),
@@ -109,21 +126,18 @@ def tile_attend_relu2_seg_kernel(tc, qT, k_words, k_scales, kb, offs, out):
             )
             return codes, scales
 
-        bias = [
-            reused.tile([P, N], F32, name="bias0", align_bytes=64, offset=29696),
-            reused.tile([P, N], F32, name="bias1", align_bytes=64, offset=17408),
-        ]
+        bias1 = reused.tile([P, N], F32, name="bias1", align_bytes=64, offset=17408)
         weight0 = sb.tile([P, N], F32, name="weight0")
         weight1 = sb.tile([P, N + 1], F32, name="weight1")
         result = [sb.tile([P, N], F32, name="result%d" % b) for b in range(B)]
         total0 = sb.tile([P, 1], F32, name="total0")
         inv = [sb.tile([P, 1], F32, name="inv%d" % b) for b in range(B)]
 
-        nc.vector.tensor_copy(bias[0][:], bias_pool[0][:].indirect(offsets[:, 0:LC]))
         pairs0 = gather_words(0)
+        nc.vector.tensor_copy(bias0[1][:], bias_pool[0][:].indirect(offsets[:, LC // 2 : LC]))
         bias_t = ps.tile([P, 4, P], F32, name="bias_t")
         for g in range(4):
-            nc.tensor.transpose(bias_t[:, g, :], bias[0][:, g * P : (g + 1) * P], identity[:])
+            nc.tensor.transpose(bias_t[:, g, :], bias0[g // 2][:, (g % 2) * P : (g % 2 + 1) * P], identity[:])
         bias_col = reused.tile([P, 4], F32, name="bias_col", align_bytes=64, offset=0)
         nc.scalar.copy(bias_col[:], bias_t[:, :, P - 1])
 
@@ -137,8 +151,8 @@ def tile_attend_relu2_seg_kernel(tc, qT, k_words, k_scales, kb, offs, out):
             for o in range(2):
                 nc.tensor.matmul_mx(
                     out=acc_t[:],
-                    lhsT=k_codes0[:, o, 2 * g * P : 2 * (g + 1) * P].bitcast(FP4X4),
-                    lhsT_scale=k_scale[o][:, g * P : (g + 1) * P],
+                    lhsT=k_codes0[g // 2][:, o, 2 * (g % 2) * P : 2 * (g % 2 + 1) * P].bitcast(FP4X4),
+                    lhsT_scale=k_scale[0][o][:, g * P : (g + 1) * P],
                     rhs=qc0[:, o * NQ : (o + 1) * NQ].bitcast(FP8X4),
                     rhs_scale=qs0[:, o * NQ : (o + 1) * NQ],
                     start=(o == 0),
@@ -155,31 +169,29 @@ def tile_attend_relu2_seg_kernel(tc, qT, k_words, k_scales, kb, offs, out):
         pairs1 = gather_words(1)
         qc1, qs1 = quantise(1)
         k_codes1 = split_words(1, pairs1)
-        half = N // 2
         acc1 = [ps.tile([P, half], F32, name="acc1%d" % h, tag="bank%d" % (3 - h)) for h in range(2)]
         for g in range(4):
-            keys = slice(g * P, (g + 1) * P)
             for o in range(2):
                 nc.tensor.matmul_mx(
                     out=acc1[g // 2][:, (g % 2) * P : (g % 2 + 1) * P],
                     lhsT=qc1[:, o * NQ : (o + 1) * NQ].bitcast(FP8X4),
                     lhsT_scale=qs1[:, o * NQ : (o + 1) * NQ],
-                    rhs=k_codes1[:, o, 2 * g * P : 2 * (g + 1) * P].bitcast(FP4X4),
-                    rhs_scale=k_scale[o][:, N + g * P : N + (g + 1) * P],
+                    rhs=k_codes1[g // 2][:, o, 2 * (g % 2) * P : 2 * (g % 2 + 1) * P].bitcast(FP4X4),
+                    rhs_scale=k_scale[1][o][:, g * P : (g + 1) * P],
                     start=(o == 0),
                     stop=(o == 1),
                 )
 
         for h in range(2):
             nc.vector.tensor_copy(
-                bias[1][:, h * half : (h + 1) * half],
+                bias1[:, h * half : (h + 1) * half],
                 bias_pool[1][:].indirect(offsets[:, LC + h * LC // 2 : LC + (h + 1) * LC // 2]),
             )
         halves = (slice(0, half), slice(half, N))
         summed = (slice(0, half), slice(half, N + 1))
         part = [sb.tile([P, 1], F32, name="part%d" % h) for h in range(2)]
         for h in range(2):
-            nc.vector.tensor_tensor(logit1[:, halves[h]], acc1[h][:], bias[1][:, halves[h]], ALU.add)
+            nc.vector.tensor_tensor(logit1[:, halves[h]], acc1[h][:], bias1[:, halves[h]], ALU.add)
         for h in range(2):
             cols = summed[h]
             nc.vector.scalar_tensor_tensor(

@@ -36,9 +36,9 @@ def tile_attend_relu2_seg_kernel(tc, qT, k_words, k_scales, kb, offs, out):
         ]
         bias_pool = [
             reused.tile([P, SEG], F32, name="bias_pool0", align_bytes=64, offset=20480),
-            sb.tile([P, T], F32, name="bias_pool1", align_bytes=64),
+            reused.tile([P, T], F32, name="bias_pool1", align_bytes=64, offset=43008),
         ]
-        scale_pool = sb.tile([P, T], U8, name="scale_pool", align_bytes=64)
+        scale_pool = reused.tile([P, T], U8, name="scale_pool", align_bytes=64, offset=43008)
         scale_listed = [sb.tile([P, N], U8, name="scale_listed%d" % b, align_bytes=64) for b in range(B)]
         k_scale = [
             [sb.tile([P, N], U8, name="k_scale%d%d" % (b, o), align_bytes=64) for o in range(2)] for b in range(B)
@@ -55,6 +55,7 @@ def tile_attend_relu2_seg_kernel(tc, qT, k_words, k_scales, kb, offs, out):
 
         nc.sync.dma_start(offsets[:], offs)
         nc.sync.dma_start(bias_pool[0][P - 1 : P, :], kb[0:1, 0:SEG])
+        nc.vector.memset(scale_pool[:].bitcast(I32), 0)
         for e in range(2):
             nc.sync.dma_start(scale_pool[16 + 32 * e : 32 + 32 * e, :].bitcast(I32), scale_rows[e].bitcast(I32))
         for b in range(B):
@@ -63,8 +64,6 @@ def tile_attend_relu2_seg_kernel(tc, qT, k_words, k_scales, kb, offs, out):
             nc.sync.dma_start(word_pool[b][:, cols], words_hbm[:, cols])
 
         nc.vector.memset(bias_pool[0][0 : P - 1, :], 0.0)
-        for lo, hi in ((0, 16), (32, 48), (64, P)):
-            nc.vector.memset(scale_pool[lo:hi, :].bitcast(I32), 0)
 
         one = sb.tile([P, 1], F32, name="one")
         nc.gpsimd.memset(one[:], 1.0)
@@ -72,13 +71,12 @@ def tile_attend_relu2_seg_kernel(tc, qT, k_words, k_scales, kb, offs, out):
         make_identity(nc, identity[:])
 
         half = N // 2
-        bias0 = [
-            reused.tile([P, half], F32, name="bias0%d" % h, align_bytes=64, offset=(29696, 36864)[h]) for h in range(2)
-        ]
-        nc.vector.tensor_copy(bias0[0][:], bias_pool[0][:].indirect(offsets[:, 0 : LC // 2]))
+        bias0 = sb.tile([P, N], F32, name="bias0", align_bytes=64)
+        nc.vector.tensor_copy(bias0[:], bias_pool[0][:].indirect(offsets[:, 0:LC]))
         for b in range(B):
             nc.vector.tensor_copy(scale_listed[b][:], scale_pool[:].indirect(offsets[:, b * LC : (b + 1) * LC]))
 
+        nc.sync.dma_start(bias_pool[1][:, SEG:T], kb[:, SEG:T])
         for b, queue in enumerate((nc.scalar, nc.sync)):
             for o in range(2):
                 for h in range(2):
@@ -87,7 +85,6 @@ def tile_attend_relu2_seg_kernel(tc, qT, k_words, k_scales, kb, offs, out):
                         k_scale[b][o][64 * h : 64 * h + 64, :].bitcast(I32),
                         scale_listed[b][first : first + 64, :].bitcast(I32),
                     )
-        nc.sync.dma_start(bias_pool[1][:, SEG:T], kb[:, SEG:T])
 
         q_bf = []
         for b in range(B):
@@ -107,7 +104,7 @@ def tile_attend_relu2_seg_kernel(tc, qT, k_words, k_scales, kb, offs, out):
             k_codes = []
             for h in range(2):
                 t = reused.tile(
-                    [P, 2, N], U8, name="k_codes%d%d" % (b, h), align_bytes=64, offset=(20480, 26624)[b] + 1024 * h
+                    [P, 2, N], U8, name="k_codes%d%d" % (b, h), align_bytes=64, offset=(36864, 26624)[b] + 1024 * h
                 )
                 nc.vector.tensor_copy(
                     t[:].rearrange("p o c -> p (o c)").bitcast(U16).rearrange("p (o n) -> p o n", o=2),
@@ -134,10 +131,9 @@ def tile_attend_relu2_seg_kernel(tc, qT, k_words, k_scales, kb, offs, out):
         inv = [sb.tile([P, 1], F32, name="inv%d" % b) for b in range(B)]
 
         pairs0 = gather_words(0)
-        nc.vector.tensor_copy(bias0[1][:], bias_pool[0][:].indirect(offsets[:, LC // 2 : LC]))
         bias_t = ps.tile([P, 4, P], F32, name="bias_t")
         for g in range(4):
-            nc.tensor.transpose(bias_t[:, g, :], bias0[g // 2][:, (g % 2) * P : (g % 2 + 1) * P], identity[:])
+            nc.tensor.transpose(bias_t[:, g, :], bias0[:, g * P : (g + 1) * P], identity[:])
         bias_col = reused.tile([P, 4], F32, name="bias_col", align_bytes=64, offset=0)
         nc.scalar.copy(bias_col[:], bias_t[:, :, P - 1])
 

@@ -54,16 +54,17 @@ def tile_attend_relu2_seg_kernel(tc, qT, k_words, k_scales, kb, offs, out):
         scale_rows = k_scales.rearrange("o (h e j) t -> e (o h) j t", h=2, e=2, j=4)
 
         nc.sync.dma_start(offsets[:], offs)
+        nc.vector.memset(scale_pool[64:P, :].bitcast(I32), 0)
         nc.sync.dma_start(bias_pool[0][P - 1 : P, :], kb[0:1, 0:SEG])
-        nc.vector.memset(scale_pool[:].bitcast(I32), 0)
-        for e in range(2):
-            nc.sync.dma_start(scale_pool[16 + 32 * e : 32 + 32 * e, :].bitcast(I32), scale_rows[e].bitcast(I32))
+        nc.sync.dma_start(scale_pool[48:64, :].bitcast(I32), scale_rows[0].bitcast(I32))
+        nc.sync.dma_start(scale_pool[80:96, :].bitcast(I32), scale_rows[1].bitcast(I32))
         for b in range(B):
             cols = slice(b * SEG, (b + 1) * SEG)
             nc.sync.dma_start(q_raw[b][:], qT[b].rearrange("(o p j) q -> p o (j q)", o=2, j=4))
             nc.sync.dma_start(word_pool[b][:, cols], words_hbm[:, cols])
 
         nc.vector.memset(bias_pool[0][0 : P - 1, :], 0.0)
+        nc.vector.memset(scale_pool[0:48, :].bitcast(I32), 0)
 
         one = sb.tile([P, 1], F32, name="one")
         nc.gpsimd.memset(one[:], 1.0)
@@ -80,7 +81,7 @@ def tile_attend_relu2_seg_kernel(tc, qT, k_words, k_scales, kb, offs, out):
         for b, queue in enumerate((nc.scalar, nc.sync)):
             for o in range(2):
                 for h in range(2):
-                    first = 16 + 4 * (2 * o + h)
+                    first = 48 + 4 * (2 * o + h)
                     queue.dma_start(
                         k_scale[b][o][64 * h : 64 * h + 64, :].bitcast(I32),
                         scale_listed[b][first : first + 64, :].bitcast(I32),

@@ -125,10 +125,10 @@ def tile_attend_relu2_seg_kernel(tc, qT, k_words, k_scales, kb, offs, out):
             return codes, scales
 
         bias1 = reused.tile([P, N], F32, name="bias1", align_bytes=64, offset=17408)
-        weight0 = sb.tile([P, N], F32, name="weight0")
+        weight0 = [sb.tile([P, half + 1], F32, name="weight0%d" % h) for h in range(2)]
         weight1 = sb.tile([P, N + 1], F32, name="weight1")
         result = [sb.tile([P, N], F32, name="result%d" % b) for b in range(B)]
-        total0 = sb.tile([P, 1], F32, name="total0")
+        part0 = [sb.tile([P, 1], F32, name="part0%d" % h) for h in range(2)]
         inv = [sb.tile([P, 1], F32, name="inv%d" % b) for b in range(B)]
 
         pairs0 = gather_words(0)
@@ -142,7 +142,8 @@ def tile_attend_relu2_seg_kernel(tc, qT, k_words, k_scales, kb, offs, out):
         k_codes0 = split_words(0, pairs0)
 
         relu_t = sb.tile([P, 4, NQ], F32, name="relu_t")
-        relu0 = ps.tile([P, N], F32, name="relu0")
+        relu0 = [ps.tile([P, half + P], F32, name="relu00"), ps.tile([P, half], F32, name="relu01")]
+        nc.tensor.transpose(relu0[0][:, half : half + P], one[:].to_broadcast([P, P]), identity[:])
         for g in range(4):
             acc_t = ps.tile([P, NQ], F32, name="acc_t%d" % g, tag="bank%d" % g)
             for o in range(2):
@@ -157,11 +158,15 @@ def tile_attend_relu2_seg_kernel(tc, qT, k_words, k_scales, kb, offs, out):
                 )
             nc.scalar.activation(relu_t[:, g, :], acc_t[:], ACT.Relu, bias=bias_col[:, g : g + 1])
         for g in range(4):
-            nc.tensor.transpose(relu0[:, g * P : (g + 1) * P], relu_t[:, g, :], identity[:])
-        nc.scalar.activation(weight0[:], relu0[:], ACT.Square, accum_out=total0[:])
-        nc.scalar.activation(inv[0][:], total0[:], ACT.Abs_reciprocal_sqrt, bias=1.0)
-        nc.scalar.activation(result[0][:], relu0[:], ACT.Square, scale=inv[0][:])
-        nc.sync.dma_start(out[0], result[0][:])
+            nc.tensor.transpose(relu0[g // 2][:, (g % 2) * P : (g % 2 + 1) * P], relu_t[:, g, :], identity[:])
+        halves = (slice(0, half), slice(half, N))
+        for h in range(2):
+            width = half + 1 - h
+            nc.scalar.activation(weight0[h][:, 0:width], relu0[h][:, 0:width], ACT.Square, accum_out=part0[h][:])
+        nc.scalar.activation(inv[0][:], part0[1][:], ACT.Abs_reciprocal_sqrt, bias=part0[0][:])
+        for h in range(2):
+            nc.scalar.activation(result[0][:, halves[h]], relu0[h][:, 0:half], ACT.Square, scale=inv[0][:])
+            nc.sync.dma_start(out[0][:, halves[h]], result[0][:, halves[h]])
 
         pairs1 = gather_words(1)
         qc1, qs1 = quantise(1)
@@ -184,7 +189,6 @@ def tile_attend_relu2_seg_kernel(tc, qT, k_words, k_scales, kb, offs, out):
                 bias1[:, h * half : (h + 1) * half],
                 bias_pool[1][:].indirect(offsets[:, LC + h * LC // 2 : LC + (h + 1) * LC // 2]),
             )
-        halves = (slice(0, half), slice(half, N))
         summed = (slice(0, half), slice(half, N + 1))
         part = [sb.tile([P, 1], F32, name="part%d" % h) for h in range(2)]
         for h in range(2):
@@ -195,7 +199,7 @@ def tile_attend_relu2_seg_kernel(tc, qT, k_words, k_scales, kb, offs, out):
                 weight1[:, cols], logit1[:, cols], 0.0, logit1[:, cols], ALU.max, ALU.mult, accum_out=part[h][:]
             )
         nc.scalar.activation(inv[1][:], part[1][:], ACT.Abs_reciprocal_sqrt, bias=part[0][:])
-        for h, queue in enumerate((nc.sync, nc.scalar)):
-            cols = halves[h]
+        pieces = (slice(0, 128), slice(128, 320), slice(320, N))
+        for cols, queue in zip(pieces, (nc.sync, nc.scalar, nc.sync)):
             nc.vector.tensor_scalar(result[1][:, cols], weight1[:, cols], inv[1][:], inv[1][:], ALU.mult, ALU.mult)
             queue.dma_start(out[1][:, cols], result[1][:, cols])

@@ -199,7 +199,6 @@ def tile_attend_relu2_seg_kernel(tc, qT, k_words, k_scales, kb, offs, out):
                 weight1[:, cols], logit1[:, cols], 0.0, logit1[:, cols], ALU.max, ALU.mult, accum_out=part[h][:]
             )
         nc.scalar.activation(inv[1][:], part[1][:], ACT.Abs_reciprocal_sqrt, bias=part[0][:])
-        pieces = (slice(0, 128), slice(128, 320), slice(320, N))
-        for cols, queue in zip(pieces, (nc.sync, nc.scalar, nc.sync)):
+        for cols, queue in zip(halves, (nc.sync, nc.scalar)):
             nc.vector.tensor_scalar(result[1][:, cols], weight1[:, cols], inv[1][:], inv[1][:], ALU.mult, ALU.mult)
             queue.dma_start(out[1][:, cols], result[1][:, cols])

@@ -103,15 +103,20 @@ def tile_attend_relu2_seg_kernel(tc, qT, k_words, k_scales, kb, offs, out):
 
         def split_words(b, pairs):
             k_codes = []
-            for h in range(2):
+            for first, groups in ((0, 1), (1, 1), (2, 2)):
+                keys = groups * P
                 t = reused.tile(
-                    [P, 2, N], U8, name="k_codes%d%d" % (b, h), align_bytes=64, offset=(36864, 26624)[b] + 1024 * h
+                    [P, 2, 2 * keys],
+                    U8,
+                    name="k_codes%d%d" % (b, first),
+                    align_bytes=64,
+                    offset=(36864, 26624)[b] + 512 * first,
                 )
                 nc.vector.tensor_copy(
                     t[:].rearrange("p o c -> p (o c)").bitcast(U16).rearrange("p (o n) -> p o n", o=2),
-                    pairs[:, h * N // 2 : (h + 1) * N // 2].bitcast(U16).rearrange("p (n o) -> p o n", o=2),
+                    pairs[:, first * P : first * P + keys].bitcast(U16).rearrange("p (n o) -> p o n", o=2),
                 )
-                k_codes.append(t)
+                k_codes.extend([[t[:, o, 2 * g * P : 2 * (g + 1) * P] for o in range(2)] for g in range(groups)])
             return k_codes
 
         def quantise(b):
@@ -149,7 +154,7 @@ def tile_attend_relu2_seg_kernel(tc, qT, k_words, k_scales, kb, offs, out):
             for o in range(2):
                 nc.tensor.matmul_mx(
                     out=acc_t[:],
-                    lhsT=k_codes0[g // 2][:, o, 2 * (g % 2) * P : 2 * (g % 2 + 1) * P].bitcast(FP4X4),
+                    lhsT=k_codes0[g][o].bitcast(FP4X4),
                     lhsT_scale=k_scale[0][o][:, g * P : (g + 1) * P],
                     rhs=qc0[:, o * NQ : (o + 1) * NQ].bitcast(FP8X4),
                     rhs_scale=qs0[:, o * NQ : (o + 1) * NQ],
@@ -166,7 +171,7 @@ def tile_attend_relu2_seg_kernel(tc, qT, k_words, k_scales, kb, offs, out):
         nc.scalar.activation(inv[0][:], part0[1][:], ACT.Abs_reciprocal_sqrt, bias=part0[0][:])
         for h in range(2):
             nc.scalar.activation(result[0][:, halves[h]], relu0[h][:, 0:half], ACT.Square, scale=inv[0][:])
-            nc.sync.dma_start(out[0][:, halves[h]], result[0][:, halves[h]])
+        nc.sync.dma_start(out[0], result[0][:])
 
         pairs1 = gather_words(1)
         qc1, qs1 = quantise(1)
@@ -178,7 +183,7 @@ def tile_attend_relu2_seg_kernel(tc, qT, k_words, k_scales, kb, offs, out):
                     out=acc1[g // 2][:, (g % 2) * P : (g % 2 + 1) * P],
                     lhsT=qc1[:, o * NQ : (o + 1) * NQ].bitcast(FP8X4),
                     lhsT_scale=qs1[:, o * NQ : (o + 1) * NQ],
-                    rhs=k_codes1[g // 2][:, o, 2 * (g % 2) * P : 2 * (g % 2 + 1) * P].bitcast(FP4X4),
+                    rhs=k_codes1[g][o].bitcast(FP4X4),
                     rhs_scale=k_scale[1][o][:, g * P : (g + 1) * P],
                     start=(o == 0),
                     stop=(o == 1),

@@ -204,6 +204,6 @@ def tile_attend_relu2_seg_kernel(tc, qT, k_words, k_scales, kb, offs, out):
                 weight1[:, cols], logit1[:, cols], 0.0, logit1[:, cols], ALU.max, ALU.mult, accum_out=part[h][:]
             )
         nc.scalar.activation(inv[1][:], part[1][:], ACT.Abs_reciprocal_sqrt, bias=part[0][:])
-        for cols, queue in zip(halves, (nc.sync, nc.scalar)):
+        for cols, queue in zip(halves, (nc.scalar, nc.scalar)):
             nc.vector.tensor_scalar(result[1][:, cols], weight1[:, cols], inv[1][:], inv[1][:], ALU.mult, ALU.mult)
             queue.dma_start(out[1][:, cols], result[1][:, cols])

@@ -204,6 +204,7 @@ def tile_attend_relu2_seg_kernel(tc, qT, k_words, k_scales, kb, offs, out):
                 weight1[:, cols], logit1[:, cols], 0.0, logit1[:, cols], ALU.max, ALU.mult, accum_out=part[h][:]
             )
         nc.scalar.activation(inv[1][:], part[1][:], ACT.Abs_reciprocal_sqrt, bias=part[0][:])
-        for cols, queue in zip(halves, (nc.scalar, nc.scalar)):
+        pieces = (slice(0, P), slice(P, half), slice(half, N))
+        for cols, queue in zip(pieces, (nc.sync, nc.scalar, nc.scalar)):
             nc.vector.tensor_scalar(result[1][:, cols], weight1[:, cols], inv[1][:], inv[1][:], ALU.mult, ALU.mult)
             queue.dma_start(out[1][:, cols], result[1][:, cols])

@@ -73,7 +73,7 @@ def tile_attend_relu2_seg_kernel(tc, qT, k_words, k_scales, kb, offs, out):
 
         half = N // 2
         bias0 = sb.tile([P, N], F32, name="bias0", align_bytes=64)
-        nc.vector.tensor_copy(bias0[:], bias_pool[0][:].indirect(offsets[:, 0:LC]))
+        nc.scalar.activation(bias0[:], bias_pool[0][:].indirect(offsets[:, 0:LC]), ACT.Copy)
         for b in range(B):
             nc.vector.tensor_copy(scale_listed[b][:], scale_pool[:].indirect(offsets[:, b * LC : (b + 1) * LC]))
 

@@ -129,7 +129,10 @@ def tile_attend_relu2_seg_kernel(tc, qT, k_words, k_scales, kb, offs, out):
             )
             return codes, scales
 
-        bias1 = reused.tile([P, N], F32, name="bias1", align_bytes=64, offset=17408)
+        bias1 = [
+            reused.tile([P, half], F32, name="bias1%d" % h, align_bytes=64, offset=(36864 + 1024, 17408)[h])
+            for h in range(2)
+        ]
         weight0 = [sb.tile([P, half + 1], F32, name="weight0%d" % h) for h in range(2)]
         weight1 = sb.tile([P, N + 1], F32, name="weight1")
         result = [sb.tile([P, N], F32, name="result%d" % b) for b in range(B)]
@@ -164,6 +167,7 @@ def tile_attend_relu2_seg_kernel(tc, qT, k_words, k_scales, kb, offs, out):
             nc.scalar.activation(relu_t[:, g, :], acc_t[:], ACT.Relu, bias=bias_col[:, g : g + 1])
         for g in range(4):
             nc.tensor.transpose(relu0[g // 2][:, (g % 2) * P : (g % 2 + 1) * P], relu_t[:, g, :], identity[:])
+        nc.scalar.activation(bias1[0][:], bias_pool[1][:].indirect(offsets[:, LC : LC + LC // 2]), ACT.Copy)
         halves = (slice(0, half), slice(half, N))
         for h in range(2):
             width = half + 1 - h
@@ -189,15 +193,11 @@ def tile_attend_relu2_seg_kernel(tc, qT, k_words, k_scales, kb, offs, out):
                     stop=(o == 1),
                 )
 
-        for h in range(2):
-            nc.vector.tensor_copy(
-                bias1[:, h * half : (h + 1) * half],
-                bias_pool[1][:].indirect(offsets[:, LC + h * LC // 2 : LC + (h + 1) * LC // 2]),
-            )
+        nc.vector.tensor_copy(bias1[1][:], bias_pool[1][:].indirect(offsets[:, LC + LC // 2 : 2 * LC]))
         summed = (slice(0, half), slice(half, N + 1))
         part = [sb.tile([P, 1], F32, name="part%d" % h) for h in range(2)]
         for h in range(2):
-            nc.vector.tensor_tensor(logit1[:, halves[h]], acc1[h][:], bias1[:, halves[h]], ALU.add)
+            nc.vector.tensor_tensor(logit1[:, halves[h]], acc1[h][:], bias1[h][:], ALU.add)
         for h in range(2):
             cols = summed[h]
             nc.vector.scalar_tensor_tensor(

@@ -43,7 +43,6 @@ def tile_attend_relu2_seg_kernel(tc, qT, k_words, k_scales, kb, offs, out):
         k_scale = [
             [sb.tile([P, N], U8, name="k_scale%d%d" % (b, o), align_bytes=64) for o in range(2)] for b in range(B)
         ]
-        identity = sb.tile([P, P], F32, name="identity")
         logit1 = sb.tile([P, N + 1], F32, name="logit1")
         q_raw = [
             reused.tile([P, 2, 4 * NQ], F32, name="q_raw0", align_bytes=64, offset=36864),
@@ -54,7 +53,6 @@ def tile_attend_relu2_seg_kernel(tc, qT, k_words, k_scales, kb, offs, out):
         scale_rows = k_scales.rearrange("o (h e j) t -> e (o h) j t", h=2, e=2, j=4)
 
         nc.sync.dma_start(offsets[:], offs)
-        nc.vector.memset(scale_pool[64:P, :].bitcast(I32), 0)
         nc.sync.dma_start(bias_pool[0][P - 1 : P, :], kb[0:1, 0:SEG])
         nc.sync.dma_start(scale_pool[48:64, :].bitcast(I32), scale_rows[0].bitcast(I32))
         nc.sync.dma_start(scale_pool[80:96, :].bitcast(I32), scale_rows[1].bitcast(I32))
@@ -64,16 +62,18 @@ def tile_attend_relu2_seg_kernel(tc, qT, k_words, k_scales, kb, offs, out):
             nc.sync.dma_start(word_pool[b][:, cols], words_hbm[:, cols])
 
         nc.vector.memset(bias_pool[0][0 : P - 1, :], 0.0)
-        nc.vector.memset(scale_pool[0:48, :].bitcast(I32), 0)
+        for first, end in ((0, 48), (64, 80), (96, P)):
+            nc.vector.memset(scale_pool[first:end, :].bitcast(I32), 0)
 
         one = sb.tile([P, 1], F32, name="one")
         nc.gpsimd.memset(one[:], 1.0)
         nc.scalar.activation(logit1[:, N : N + 1], one[:], ACT.Abs_reciprocal_sqrt)
-        make_identity(nc, identity[:])
 
         half = N // 2
-        bias0 = sb.tile([P, N], F32, name="bias0", align_bytes=64)
+        bias0 = reused.tile([P, N], F32, name="bias0", align_bytes=64, offset=31744)
         nc.scalar.activation(bias0[:], bias_pool[0][:].indirect(offsets[:, 0:LC]), ACT.Copy)
+        identity = reused.tile([P, P], F32, name="identity", align_bytes=64, offset=20480)
+        make_identity(nc, identity[:])
         for b in range(B):
             nc.vector.tensor_copy(scale_listed[b][:], scale_pool[:].indirect(offsets[:, b * LC : (b + 1) * LC]))
 
@@ -110,7 +110,7 @@ def tile_attend_relu2_seg_kernel(tc, qT, k_words, k_scales, kb, offs, out):
                     U8,
                     name="k_codes%d%d" % (b, first),
                     align_bytes=64,
-                    offset=(36864, 26624)[b] + 512 * first,
+                    offset=(32000, 26624)[b] + 512 * first,
                 )
                 nc.vector.tensor_copy(
                     t[:].rearrange("p o c -> p (o c)").bitcast(U16).rearrange("p (o n) -> p o n", o=2),
@@ -120,7 +120,7 @@ def tile_attend_relu2_seg_kernel(tc, qT, k_words, k_scales, kb, offs, out):
             return k_codes
 
         def quantise(b):
-            codes = reused.tile([P, 2 * NQ], U32, name="q_codes%d" % b, align_bytes=64, offset=(40960, 28672)[b])
+            codes = reused.tile([P, 2 * NQ], U32, name="q_codes%d" % b, align_bytes=64, offset=(30976, 9216)[b])
             scales = sb.tile([P, 2 * NQ], U8, name="q_scales%d" % b, align_bytes=64)
             nc.vector.quantize_mx(
                 out=codes[:].bitcast(FP8X4),
@@ -130,7 +130,7 @@ def tile_attend_relu2_seg_kernel(tc, qT, k_words, k_scales, kb, offs, out):
             return codes, scales
 
         bias1 = [
-            reused.tile([P, half], F32, name="bias1%d" % h, align_bytes=64, offset=(36864 + 1024, 17408)[h])
+            reused.tile([P, half], F32, name="bias1%d" % h, align_bytes=64, offset=(32000 + 1024, 17408)[h])
             for h in range(2)
         ]
         weight0 = [sb.tile([P, half + 1], F32, name="weight0%d" % h) for h in range(2)]

@@ -52,10 +52,10 @@ def tile_attend_relu2_seg_kernel(tc, qT, k_words, k_scales, kb, offs, out):
         words_hbm = k_words[0].rearrange("p t c -> p (t c)").bitcast(I32)
         scale_rows = k_scales.rearrange("o (h e j) t -> e (o h) j t", h=2, e=2, j=4)
 
-        nc.sync.dma_start(offsets[:], offs)
-        nc.sync.dma_start(bias_pool[0][P - 1 : P, :], kb[0:1, 0:SEG])
         nc.sync.dma_start(scale_pool[48:64, :].bitcast(I32), scale_rows[0].bitcast(I32))
         nc.sync.dma_start(scale_pool[80:96, :].bitcast(I32), scale_rows[1].bitcast(I32))
+        nc.sync.dma_start(bias_pool[0][P - 1 : P, :], kb[0:1, 0:SEG])
+        nc.sync.dma_start(offsets[:], offs)
         for b in range(B):
             cols = slice(b * SEG, (b + 1) * SEG)
             nc.sync.dma_start(q_raw[b][:], qT[b].rearrange("(o p j) q -> p o (j q)", o=2, j=4))

from contextlib import ExitStack

import concourse.mybir as mybir
from concourse.masks import make_identity

B, N, T, D, NQ = 2, 512, 2048, 1024, 128
FLOPS = 2 * B * N * D * NQ

F32 = mybir.dt.float32
BF16 = mybir.dt.bfloat16
I32 = mybir.dt.int32
U32 = mybir.dt.uint32
U16 = mybir.dt.uint16
U8 = mybir.dt.uint8
FP8X4 = mybir.dt.float8_e4m3fn_x4
FP4X4 = mybir.dt.float4_e2m1fn_x4
ALU = mybir.AluOpType
ACT = mybir.ActivationFunctionType

P = 128
SEG = T // B
LC = N // 16


def tile_attend_relu2_seg_kernel(tc, qT, k_words, k_scales, kb, offs, out):
    nc = tc.nc
    with ExitStack() as ctx:
        sb = ctx.enter_context(tc.tile_pool(name="sb", bufs=1))
        ps = ctx.enter_context(tc.psum_pool(name="ps", bufs=1))
        reused = ctx.enter_context(tc.tile_pool(name="reused", bufs=1))

        offsets = sb.tile([P, B * LC], U16, name="offsets")
        word_pool = [
            reused.tile([P, (b + 1) * SEG], I32, name="word_pool%d" % b, align_bytes=64, offset=(4096, 10240)[b])
            for b in range(B)
        ]
        bias_pool = [
            reused.tile([P, SEG], F32, name="bias_pool0", align_bytes=64, offset=20480),
            reused.tile([P, T], F32, name="bias_pool1", align_bytes=64, offset=43008),
        ]
        scale_pool = reused.tile([P, T], U8, name="scale_pool", align_bytes=64, offset=43008)
        scale_listed = [sb.tile([P, N], U8, name="scale_listed%d" % b, align_bytes=64) for b in range(B)]
        k_scale = [
            [sb.tile([P, N], U8, name="k_scale%d%d" % (b, o), align_bytes=64) for o in range(2)] for b in range(B)
        ]
        logit1 = sb.tile([P, N + 1], F32, name="logit1")
        q_raw = [
            reused.tile([P, 2, 4 * NQ], F32, name="q_raw0", align_bytes=64, offset=36864),
            reused.tile([P, 2, 4 * NQ], F32, name="q_raw1", align_bytes=64, offset=0),
        ]

        words_hbm = k_words[0].rearrange("p t c -> p (t c)").bitcast(I32)
        scale_rows = k_scales.rearrange("o (h e j) t -> e (o h) j t", h=2, e=2, j=4)

        nc.sync.dma_start(scale_pool[48:64, :].bitcast(I32), scale_rows[0].bitcast(I32))
        nc.sync.dma_start(scale_pool[80:96, :].bitcast(I32), scale_rows[1].bitcast(I32))
        nc.sync.dma_start(bias_pool[0][P - 1 : P, :], kb[0:1, 0:SEG])
        nc.sync.dma_start(offsets[:], offs)
        for b in range(B):
            cols = slice(b * SEG, (b + 1) * SEG)
            nc.sync.dma_start(q_raw[b][:], qT[b].rearrange("(o p j) q -> p o (j q)", o=2, j=4))
            nc.sync.dma_start(word_pool[b][:, cols], words_hbm[:, cols])

        nc.vector.memset(bias_pool[0][0 : P - 1, :], 0.0)
        for first, end in ((0, 48), (64, 80), (96, P)):
            nc.vector.memset(scale_pool[first:end, :].bitcast(I32), 0)

        one = sb.tile([P, 1], F32, name="one")
        nc.gpsimd.memset(one[:], 1.0)
        nc.scalar.activation(logit1[:, N : N + 1], one[:], ACT.Abs_reciprocal_sqrt)

        half = N // 2
        bias0 = reused.tile([P, N], F32, name="bias0", align_bytes=64, offset=31744)
        nc.scalar.activation(bias0[:], bias_pool[0][:].indirect(offsets[:, 0:LC]), ACT.Copy)
        identity = reused.tile([P, P], F32, name="identity", align_bytes=64, offset=20480)
        make_identity(nc, identity[:])
        for b in range(B):
            nc.vector.tensor_copy(scale_listed[b][:], scale_pool[:].indirect(offsets[:, b * LC : (b + 1) * LC]))

        nc.sync.dma_start(bias_pool[1][:, SEG:T], kb[:, SEG:T])
        for b, queue in enumerate((nc.scalar, nc.sync)):
            for o in range(2):
                for h in range(2):
                    first = 48 + 4 * (2 * o + h)
                    queue.dma_start(
                        k_scale[b][o][64 * h : 64 * h + 64, :].bitcast(I32),
                        scale_listed[b][first : first + 64, :].bitcast(I32),
                    )

        q_bf = []
        for b in range(B):
            t = reused.tile([P, 2, NQ, 4], BF16, name="q_bf%d" % b, align_bytes=64, offset=(8192, 18432)[b])
            nc.scalar.copy(
                t[:].rearrange("p o (c i) j -> p o c j i", i=4),
                q_raw[b][:].rearrange("p o (j c i) -> p o c j i", j=4, i=4),
            )
            q_bf.append(t)

        def gather_words(b):
            pairs = reused.tile([P, N], U32, name="pairs%d" % b, align_bytes=64, offset=(24576, 7168)[b])
            nc.vector.tensor_copy(pairs[:], word_pool[b][:].bitcast(U32).indirect(offsets[:, b * LC : (b + 1) * LC]))
            return pairs

        def split_words(b, pairs):
            k_codes = []
            for first, groups in ((0, 1), (1, 1), (2, 2)):
                keys = groups * P
                t = reused.tile(
                    [P, 2, 2 * keys],
                    U8,
                    name="k_codes%d%d" % (b, first),
                    align_bytes=64,
                    offset=(32000, 26624)[b] + 512 * first,
                )
                nc.vector.tensor_copy(
                    t[:].rearrange("p o c -> p (o c)").bitcast(U16).rearrange("p (o n) -> p o n", o=2),
                    pairs[:, first * P : first * P + keys].bitcast(U16).rearrange("p (n o) -> p o n", o=2),
                )
                k_codes.extend([[t[:, o, 2 * g * P : 2 * (g + 1) * P] for o in range(2)] for g in range(groups)])
            return k_codes

        def quantise(b):
            codes = reused.tile([P, 2 * NQ], U32, name="q_codes%d" % b, align_bytes=64, offset=(30976, 9216)[b])
            scales = sb.tile([P, 2 * NQ], U8, name="q_scales%d" % b, align_bytes=64)
            nc.vector.quantize_mx(
                out=codes[:].bitcast(FP8X4),
                scales=scales[:],
                in_=q_bf[b][:].rearrange("p o q j -> p (o q j)"),
            )
            return codes, scales

        bias1 = [
            reused.tile([P, half], F32, name="bias1%d" % h, align_bytes=64, offset=(32000 + 1024, 17408)[h])
            for h in range(2)
        ]
        weight0 = [sb.tile([P, half + 1], F32, name="weight0%d" % h) for h in range(2)]
        weight1 = sb.tile([P, N + 1], F32, name="weight1")
        result = [sb.tile([P, N], F32, name="result%d" % b) for b in range(B)]
        part0 = [sb.tile([P, 1], F32, name="part0%d" % h) for h in range(2)]
        inv = [sb.tile([P, 1], F32, name="inv%d" % b) for b in range(B)]

        pairs0 = gather_words(0)
        bias_t = ps.tile([P, 4, P], F32, name="bias_t")
        for g in range(4):
            nc.tensor.transpose(bias_t[:, g, :], bias0[:, g * P : (g + 1) * P], identity[:])
        bias_col = reused.tile([P, 4], F32, name="bias_col", align_bytes=64, offset=0)
        nc.scalar.copy(bias_col[:], bias_t[:, :, P - 1])

        qc0, qs0 = quantise(0)
        k_codes0 = split_words(0, pairs0)

        relu_t = sb.tile([P, 4, NQ], F32, name="relu_t")
        relu0 = [ps.tile([P, half + P], F32, name="relu00"), ps.tile([P, half], F32, name="relu01")]
        nc.tensor.transpose(relu0[0][:, half : half + P], one[:].to_broadcast([P, P]), identity[:])
        for g in range(4):
            acc_t = ps.tile([P, NQ], F32, name="acc_t%d" % g, tag="bank%d" % g)
            for o in range(2):
                nc.tensor.matmul_mx(
                    out=acc_t[:],
                    lhsT=k_codes0[g][o].bitcast(FP4X4),
                    lhsT_scale=k_scale[0][o][:, g * P : (g + 1) * P],
                    rhs=qc0[:, o * NQ : (o + 1) * NQ].bitcast(FP8X4),
                    rhs_scale=qs0[:, o * NQ : (o + 1) * NQ],
                    start=(o == 0),
                    stop=(o == 1),
                )
            nc.scalar.activation(relu_t[:, g, :], acc_t[:], ACT.Relu, bias=bias_col[:, g : g + 1])
        for g in range(4):
            nc.tensor.transpose(relu0[g // 2][:, (g % 2) * P : (g % 2 + 1) * P], relu_t[:, g, :], identity[:])
        nc.scalar.activation(bias1[0][:], bias_pool[1][:].indirect(offsets[:, LC : LC + LC // 2]), ACT.Copy)
        halves = (slice(0, half), slice(half, N))
        for h in range(2):
            width = half + 1 - h
            nc.scalar.activation(weight0[h][:, 0:width], relu0[h][:, 0:width], ACT.Square, accum_out=part0[h][:])
        nc.scalar.activation(inv[0][:], part0[1][:], ACT.Abs_reciprocal_sqrt, bias=part0[0][:])
        for h in range(2):
            nc.scalar.activation(result[0][:, halves[h]], relu0[h][:, 0:half], ACT.Square, scale=inv[0][:])
        nc.sync.dma_start(out[0], result[0][:])

        pairs1 = gather_words(1)
        qc1, qs1 = quantise(1)
        k_codes1 = split_words(1, pairs1)
        acc1 = [ps.tile([P, half], F32, name="acc1%d" % h, tag="bank%d" % (3 - h)) for h in range(2)]
        for g in range(4):
            for o in range(2):
                nc.tensor.matmul_mx(
                    out=acc1[g // 2][:, (g % 2) * P : (g % 2 + 1) * P],
                    lhsT=qc1[:, o * NQ : (o + 1) * NQ].bitcast(FP8X4),
                    lhsT_scale=qs1[:, o * NQ : (o + 1) * NQ],
                    rhs=k_codes1[g][o].bitcast(FP4X4),
                    rhs_scale=k_scale[1][o][:, g * P : (g + 1) * P],
                    start=(o == 0),
                    stop=(o == 1),
                )

        nc.vector.tensor_copy(bias1[1][:], bias_pool[1][:].indirect(offsets[:, LC + LC // 2 : 2 * LC]))
        summed = (slice(0, half), slice(half, N + 1))
        part = [sb.tile([P, 1], F32, name="part%d" % h) for h in range(2)]
        for h in range(2):
            nc.vector.tensor_tensor(logit1[:, halves[h]], acc1[h][:], bias1[h][:], ALU.add)
        for h in range(2):
            cols = summed[h]
            nc.vector.scalar_tensor_tensor(
                weight1[:, cols], logit1[:, cols], 0.0, logit1[:, cols], ALU.max, ALU.mult, accum_out=part[h][:]
            )
        nc.scalar.activation(inv[1][:], part[1][:], ACT.Abs_reciprocal_sqrt, bias=part[0][:])
        pieces = (slice(0, P), slice(P, half), slice(half, N))
        for cols, queue in zip(pieces, (nc.sync, nc.scalar, nc.scalar)):
            nc.vector.tensor_scalar(result[1][:, cols], weight1[:, cols], inv[1][:], inv[1][:], ALU.mult, ALU.mult)
            queue.dma_start(out[1][:, cols], result[1][:, cols])
